import numpy as np
import ml_dtypes


def mxq(x, axis, fmt="e4m3"):
    dtype, down = {"e4m3": (ml_dtypes.float8_e4m3fn, 7), "e5m2": (ml_dtypes.float8_e5m2, 14)}[fmt]
    v = np.moveaxis(np.asarray(x, np.float32).astype(ml_dtypes.bfloat16).astype(np.float64), axis, -1)
    blocks = v.reshape(v.shape[:-1] + (-1, 32))
    amax = np.abs(blocks).max(-1, keepdims=True)
    byte = np.maximum(np.where(amax > 0, np.frexp(amax)[1] - 1 + 127, 0) - down, 1)
    scale = np.exp2(byte - 127.0)
    codes = (blocks / scale).astype(np.float32).astype(dtype).astype(np.float64)
    return np.moveaxis((codes * scale).reshape(v.shape), -1, axis)


WIDE = False


def mx_kscale(k):
    if not WIDE:
        return np.ones(k)
    levels = np.array([10, -10, 5, -5, 0])
    if k % 512:
        return np.exp2(np.random.permutation(np.resize(levels, k // 32))).repeat(32)
    a = np.empty((k // 512, 16))
    for p in range(k // 512):
        a[p, :8] = np.random.permutation(np.resize(levels, 8))
        for g in range(8):
            far = levels[np.abs(levels - a[p, g]) >= 10]
            a[p, g + 8] = far[np.random.randint(len(far))]
    return np.exp2(a.ravel()).repeat(32)


def f64(x):
    return np.asarray(x).astype(np.float64)


def striped(idx):
    return np.tile(idx.reshape(-1, 16).T, (8, 1)).astype(np.uint16)


def unstriped(offs):
    return offs[:16].T.reshape(-1).astype(np.int64)


def pack_weight(w):
    k, n = w.shape
    w = f64(np.asarray(w, np.float32).astype(ml_dtypes.bfloat16)).reshape(k // 32, 32, n)
    amax = np.abs(w).max(1)
    byte = np.clip(np.where(amax > 0, np.frexp(amax)[1] - 1 + 127 - 7, 1), 1, 254)
    scaled = (w * np.exp2(127.0 - byte)[:, None, :]).reshape(k, n).astype(np.float32)
    words = np.ascontiguousarray(scaled.reshape(k // 512, 128, 4, n).transpose(0, 1, 3, 2)).astype(ml_dtypes.float8_e4m3fn).view(np.uint8)
    return words, np.ascontiguousarray(byte.astype(np.uint8).reshape(k // 512, 16, n))


def unpack_weight(words, scales):
    g, p, n, _ = words.shape
    vals = np.ascontiguousarray(words).view(ml_dtypes.float8_e4m3fn).astype(np.float64) * np.repeat(np.exp2(scales.astype(np.float64) - 127.0), 8, axis=1)[..., None]
    return vals.transpose(0, 1, 3, 2).reshape(g * 512, n)


K, T, S, N, U = 512, 2048, 512, 128, 512
P = 2 ** 7


def setup_inputs():
    n = np.random.standard_normal
    s = mx_kscale(K)[:, None]
    near = np.random.permutation(np.concatenate([np.arange(S), np.arange(S)]))
    packed_xT = pack_weight(n((K, T)) * s)
    return {
        "x_words": packed_xT[0],
        "x_scales": packed_xT[1],
        "w1": (n((K, N)) / np.sqrt(K) / s).astype(np.float32),
        "w2": (n((K, N)) / np.sqrt(K) / s).astype(np.float32),
        "eps": (np.tile(np.random.uniform(0.3, 1.5, S), (P, 1))).astype(np.float32),
        "sig": (np.tile(np.random.uniform(0.4, 0.8, S), (P, 1))).astype(np.float32),
        "offs": striped(np.random.permutation(T)[:S]),
        "ia": striped(near[:U]),
        "ib": striped(near[U:]),
    }


def reference(x_words, x_scales, w1, w2, eps, sig, offs, ia, ib):
    sg = f64(sig)[:1][:, unstriped(ia)] + f64(sig)[:1][:, unstriped(ib)]
    xq = unpack_weight(x_words, x_scales)[:, unstriped(offs)]
    y = mxq(f64(w1), 0, "e4m3").T @ xq
    dx = y[:, unstriped(ia)] - y[:, unstriped(ib)]
    z = mxq(f64(w2), 0, "e4m3").T @ xq
    dy = z[:, unstriped(ia)] - z[:, unstriped(ib)]
    rsq = (dx) ** 2 + (dy) ** 2 + 0.8
    qr = ((sg) ** 2) / rsq
    q6 = ((qr) ** 2) * qr
    return ((((f64(eps)[:1][:, unstriped(ia)]) * (f64(eps)[:1][:, unstriped(ib)])) * (12.0 * ((q6) ** 2) - (6.0 * q6))) * dx) / rsq

@@ -1,0 +1,164 @@
+from contextlib import ExitStack
+
+import concourse.mybir as mybir
+from concourse.masks import make_identity
+
+F32 = mybir.dt.float32
+BF16 = mybir.dt.bfloat16
+I32 = mybir.dt.int32
+U32 = mybir.dt.uint32
+U16 = mybir.dt.uint16
+U8 = mybir.dt.uint8
+FP8X4 = mybir.dt.float8_e4m3fn_x4
+ALU = mybir.AluOpType
+ACT = mybir.ActivationFunctionType
+
+K, T, S, M, U = 512, 2048, 512, 128, 512
+P = 128
+PACK = 4
+LANES = 16
+HALF = S // 2
+CHUNK = 128
+CHUNKS = U // CHUNK
+SOFTENING = 0.8
+FLOPS = 2 * 2 * K * M * S
+
+
+def entries(offsets, first, count):
+    return offsets[:, first // LANES : (first + count) // LANES]
+
+
+def tile_picked_yljmix_force_p_kernel(
+    tc, x_words, x_scales, w1, w2, eps, sig, offs, ia, ib, out
+):
+    nc = tc.nc
+    with ExitStack() as ctx:
+        keep = ctx.enter_context(tc.tile_pool(name="keep", bufs=1))
+        psum = ctx.enter_context(tc.psum_pool(name="psum", bufs=1))
+
+        offs_sb = keep.tile([P, S // LANES], U16, name="offs_sb")
+        ia_sb = keep.tile([P, U // LANES], U16, name="ia_sb")
+        ib_sb = keep.tile([P, U // LANES], U16, name="ib_sb")
+        words = keep.tile([P, T], U32, name="words", align_bytes=64)
+        scales = keep.tile([P, T], U8, name="scales", align_bytes=64)
+        params = keep.tile([P, S], F32, name="params", align_bytes=64)
+        w_raw = [keep.tile([P, PACK, M], F32, name=f"w_raw{i}", align_bytes=64) for i in range(2)]
+
+        nc.vector.memset(scales[:].bitcast(I32), 0)
+        nc.vector.memset(params[:], 0.0)
+        nc.sync.dma_start(offs_sb[:], offs)
+        nc.sync.dma_start(ia_sb[:], ia)
+        nc.sync.dma_start(ib_sb[:], ib)
+        for q in range(4):
+            nc.sync.dma_start(
+                out=scales[32 * q : 32 * q + 4, :].bitcast(I32),
+                in_=x_scales[0, 4 * q : 4 * q + 4, :].bitcast(I32),
+            )
+        nc.sync.dma_start(
+            out=words[:].bitcast(I32), in_=x_words[0].rearrange("p n t -> p (n t)").bitcast(I32)
+        )
+        nc.sync.dma_start(out=params[0:1, :], in_=eps[0:1, :])
+        nc.sync.dma_start(out=params[1:2, :], in_=sig[0:1, :])
+        for w, raw in zip((w1, w2), w_raw):
+            nc.sync.dma_start(out=raw[:], in_=w.rearrange("(p j) n -> p j n", j=PACK))
+
+        ident = keep.tile([P, P], F32, name="ident", align_bytes=64)
+        make_identity(nc, ident[:])
+        ones = keep.tile([P, P], F32, name="ones", align_bytes=64)
+        nc.gpsimd.memset(ones[:], 1.0)
+        soft = keep.tile([P, P], F32, name="soft", align_bytes=64)
+        nc.gpsimd.tensor_scalar(soft[:], ones[:], SOFTENING, 0.0, ALU.mult, ALU.add)
+        warm = keep.tile([P, 1], F32, name="warm")
+        nc.scalar.activation(warm[:], ones[:, 0:1], ACT.Abs_reciprocal_sqrt)
+
+        picked_scales = keep.tile([P, S], U8, name="picked_scales", align_bytes=64)
+        nc.vector.tensor_copy(picked_scales[:], scales[:].indirect(offs_sb[:]))
+
+        def look_up_params(name, lst, tag):
+            got = keep.tile([P, U], F32, name=f"params_{name}", align_bytes=64)
+            for h in range(2):
+                nc.vector.tensor_copy(got[:, h * HALF : (h + 1) * HALF], params[:].indirect(entries(lst, h * HALF, HALF)))
+            turned = psum.tile([P, CHUNKS, P], F32, name=f"turned_{name}", tag=tag)
+            for c in range(CHUNKS):
+                nc.tensor.transpose(turned[:, c, :], got[:, c * CHUNK : (c + 1) * CHUNK], ident[:])
+            return turned
+
+        def product(i):
+            grouped = keep.tile([P, M, PACK], BF16, name=f"grouped{i}", align_bytes=64)
+            nc.scalar.copy(out=grouped[:], in_=w_raw[i][:].rearrange("p j n -> p n j"))
+            w_codes = keep.tile([P, M], U32, name=f"w_codes{i}", align_bytes=64)
+            w_scales = keep.tile([P, M], U8, name=f"w_scales{i}", align_bytes=64)
+            nc.vector.quantize_mx(
+                out=w_codes[:].bitcast(FP8X4), scales=w_scales[:], in_=grouped[:].rearrange("p n j -> p (n j)")
+            )
+            coord = keep.tile([P, S], F32, name=f"coord{i}", align_bytes=64)
+            for h in range(2):
+                cols = slice(h * HALF, (h + 1) * HALF)
+                acc = psum.tile([P, HALF], F32, name=f"acc{i}{h}", tag=f"m{2 * i + h}")
+                nc.tensor.matmul_mx(
+                    out=acc[:],
+                    lhsT=w_codes[:].bitcast(FP8X4),
+                    lhsT_scale=w_scales[:],
+                    rhs=picked_words[h][:].bitcast(FP8X4),
+                    rhs_scale=picked_scales[:, cols],
+                    start=True,
+                    stop=True,
+                )
+                nc.scalar.copy(out=coord[:, cols], in_=acc[:])
+            return coord
+
+        ends = [look_up_params("a", ia_sb, "r2")]
+        picked_words = [keep.tile([P, HALF], U32, name=f"picked_words{h}", align_bytes=64) for h in range(2)]
+        for h in range(2):
+            nc.vector.tensor_copy(picked_words[h][:], words[:].indirect(entries(offs_sb, h * HALF, HALF)))
+        coords = [product(0), product(1)]
+        ends.append(look_up_params("b", ib_sb, "r3"))
+
+        end_a = keep.tile([P, CHUNKS, 2], F32, name="end_a")
+        nc.scalar.copy(out=end_a[:], in_=ends[0][:, :, 0:2])
+        small = {}
+        for name in ("sg", "e", "he"):
+            small[name] = keep.tile([P, CHUNKS], F32, name=name)
+        nc.vector.tensor_tensor(small["sg"][:], ends[1][:, :, 1], end_a[:, :, 1], ALU.add)
+        nc.vector.scalar_tensor_tensor(small["e"][:], ends[1][:, :, 0], -12.0, end_a[:, :, 0], ALU.mult, ALU.mult)
+        nc.vector.scalar_tensor_tensor(small["he"][:], ends[1][:, :, 0], -6.0, end_a[:, :, 0], ALU.mult, ALU.mult)
+
+        diffs, rsqs, hs = [], [], []
+        for c in range(CHUNKS):
+            first = keep.tile([P, 2, CHUNK], F32, name=f"first{c}", align_bytes=64)
+            diff = keep.tile([P, 2, CHUNK], F32, name=f"diff{c}", align_bytes=64)
+            for i in range(2):
+                nc.vector.tensor_copy(first[:, i, :], coords[i][:].indirect(entries(ia_sb, c * CHUNK, CHUNK)))
+            for i in range(2):
+                nc.vector.tensor_tensor(
+                    diff[:, i, :], coords[i][:].indirect(entries(ib_sb, c * CHUNK, CHUNK)), first[:, i, :], ALU.subtract
+                )
+            squares = keep.tile([P, 2, CHUNK], F32, name=f"squares{c}", align_bytes=64)
+            for i in range(2):
+                nc.scalar.activation(squares[:, i, :], diff[:, i, :], ACT.Square)
+            rsq = psum.tile([P, M], F32, name=f"rsq{c}", tag=f"r{c}")
+            terms = (soft[:], squares[:, 0, :], squares[:, 1, :])
+            for j, term in enumerate(terms):
+                nc.tensor.matmul(rsq[:], term, ident[:], start=(j == 0), stop=(j == len(terms) - 1), is_transpose=True)
+            r2 = keep.tile([P, M], F32, name=f"r2_{c}", align_bytes=64)
+            r4 = keep.tile([P, M], F32, name=f"r4_{c}", align_bytes=64)
+            u2 = keep.tile([P, M], F32, name=f"u2_{c}", align_bytes=64)
+            h4 = keep.tile([P, M], F32, name=f"h4_{c}", align_bytes=64)
+            nc.scalar.activation(r2[:], rsq[:], ACT.Square)
+            nc.scalar.activation(r4[:], r2[:], ACT.Abs_reciprocal_sqrt)
+            nc.scalar.activation(u2[:], r4[:], ACT.Square, scale=small["sg"][:, c : c + 1])
+            nc.scalar.activation(h4[:], u2[:], ACT.Square, scale=small["sg"][:, c : c + 1])
+            diffs.append(diff)
+            rsqs.append(rsq)
+            hs.append(h4)
+
+        for c in range(CHUNKS):
+            q = keep.tile([P, M], F32, name=f"q{c}", align_bytes=64)
+            factor = keep.tile([P, M], F32, name=f"factor{c}", align_bytes=64)
+            nc.vector.scalar_tensor_tensor(q[:], rsqs[c][:], small["e"][:, c : c + 1], hs[c][:], ALU.mult, ALU.mult)
+            nc.vector.scalar_tensor_tensor(factor[:], q[:], small["he"][:, c : c + 1], hs[c][:], ALU.subtract, ALU.mult)
+            back = psum.tile([P, CHUNK], F32, name=f"back{c}", tag=f"m{c}")
+            nc.tensor.transpose(back[:], factor[:], ident[:])
+            force = keep.tile([P, CHUNK], F32, name=f"force{c}", align_bytes=64)
+            nc.vector.tensor_tensor(force[:], back[:], diffs[c][:, 0, :], ALU.mult)
+            nc.sync.dma_start(out=out[:, c * CHUNK : (c + 1) * CHUNK], in_=force[:])

@@ -44,35 +44,33 @@ def tile_picked_yljmix_force_p_kernel(
         params = keep.tile([P, S], F32, name="params", align_bytes=64)
         w_raw = [keep.tile([P, PACK, M], F32, name=f"w_raw{i}", align_bytes=64) for i in range(2)]
 
+        nc.gpsimd.memset(params[:], 0.0)
         nc.vector.memset(scales[:].bitcast(I32), 0)
-        nc.vector.memset(params[:], 0.0)
         nc.sync.dma_start(offs_sb[:], offs)
         nc.sync.dma_start(ia_sb[:], ia)
         nc.sync.dma_start(ib_sb[:], ib)
+        nc.sync.dma_start(out=params[0:1, :], in_=eps[0:1, :])
+        nc.sync.dma_start(out=params[1:2, :], in_=sig[0:1, :])
+        nc.sync.dma_start(
+            out=words[:].bitcast(I32), in_=x_words[0].rearrange("p n t -> p (n t)").bitcast(I32)
+        )
         for q in range(4):
             nc.sync.dma_start(
                 out=scales[32 * q : 32 * q + 4, :].bitcast(I32),
                 in_=x_scales[0, 4 * q : 4 * q + 4, :].bitcast(I32),
             )
-        nc.sync.dma_start(
-            out=words[:].bitcast(I32), in_=x_words[0].rearrange("p n t -> p (n t)").bitcast(I32)
-        )
-        nc.sync.dma_start(out=params[0:1, :], in_=eps[0:1, :])
-        nc.sync.dma_start(out=params[1:2, :], in_=sig[0:1, :])
         for w, raw in zip((w1, w2), w_raw):
             nc.sync.dma_start(out=raw[:], in_=w.rearrange("(p j) n -> p j n", j=PACK))
 
         ident = keep.tile([P, P], F32, name="ident", align_bytes=64)
-        make_identity(nc, ident[:])
         ones = keep.tile([P, P], F32, name="ones", align_bytes=64)
-        nc.gpsimd.memset(ones[:], 1.0)
+        nc.vector.memset(ones[:], 1.0)
+        make_identity(nc, ident[:])
         soft = keep.tile([P, P], F32, name="soft", align_bytes=64)
-        nc.gpsimd.tensor_scalar(soft[:], ones[:], SOFTENING, 0.0, ALU.mult, ALU.add)
+        nc.vector.tensor_scalar(soft[:], ones[:], SOFTENING, None, ALU.mult)
         warm = keep.tile([P, 1], F32, name="warm")
         nc.scalar.activation(warm[:], ones[:, 0:1], ACT.Abs_reciprocal_sqrt)
 
-        picked_scales = keep.tile([P, S], U8, name="picked_scales", align_bytes=64)
-        nc.vector.tensor_copy(picked_scales[:], scales[:].indirect(offs_sb[:]))
 
         def look_up_params(name, lst, tag):
             got = keep.tile([P, U], F32, name=f"params_{name}", align_bytes=64)
@@ -83,14 +81,17 @@ def tile_picked_yljmix_force_p_kernel(
                 nc.tensor.transpose(turned[:, c, :], got[:, c * CHUNK : (c + 1) * CHUNK], ident[:])
             return turned
 
-        def product(i):
-            grouped = keep.tile([P, M, PACK], BF16, name=f"grouped{i}", align_bytes=64)
+        def quantise_weights(i):
+            grouped = keep.tile([P, M, PACK], BF16, name=f"grouped{i}", tag=f"grouped{i}", align_bytes=64)
             nc.scalar.copy(out=grouped[:], in_=w_raw[i][:].rearrange("p j n -> p n j"))
             w_codes = keep.tile([P, M], U32, name=f"w_codes{i}", align_bytes=64)
             w_scales = keep.tile([P, M], U8, name=f"w_scales{i}", align_bytes=64)
             nc.vector.quantize_mx(
                 out=w_codes[:].bitcast(FP8X4), scales=w_scales[:], in_=grouped[:].rearrange("p n j -> p (n j)")
             )
+            return w_codes, w_scales
+
+        def product(i, w_codes, w_scales):
             coord = keep.tile([P, S], F32, name=f"coord{i}", align_bytes=64)
             for h in range(2):
                 cols = slice(h * HALF, (h + 1) * HALF)
@@ -100,65 +101,86 @@ def tile_picked_yljmix_force_p_kernel(
                     lhsT=w_codes[:].bitcast(FP8X4),
                     lhsT_scale=w_scales[:],
                     rhs=picked_words[h][:].bitcast(FP8X4),
-                    rhs_scale=picked_scales[:, cols],
+                    rhs_scale=picked_scales[h][:],
                     start=True,
                     stop=True,
                 )
                 nc.scalar.copy(out=coord[:, cols], in_=acc[:])
             return coord
 
-        ends = [look_up_params("a", ia_sb, "r2")]
+        ends = [look_up_params("a", ia_sb, "r2"), look_up_params("b", ib_sb, "r3")]
         picked_words = [keep.tile([P, HALF], U32, name=f"picked_words{h}", align_bytes=64) for h in range(2)]
-        for h in range(2):
-            nc.vector.tensor_copy(picked_words[h][:], words[:].indirect(entries(offs_sb, h * HALF, HALF)))
-        coords = [product(0), product(1)]
-        ends.append(look_up_params("b", ib_sb, "r3"))
+        picked_scales = [keep.tile([P, HALF], U8, name="picked_scales0", align_bytes=64)]
+        nc.vector.tensor_copy(picked_words[0][:], words[:].indirect(entries(offs_sb, 0, HALF)))
+        nc.vector.tensor_copy(picked_scales[0][:], scales[:].indirect(entries(offs_sb, 0, HALF)))
+        nc.vector.tensor_copy(picked_words[1][:], words[:].indirect(entries(offs_sb, HALF, HALF)))
+        quantised = [quantise_weights(0)]
+        picked_scales.append(keep.tile([P, HALF], U8, name="picked_scales1", tag="grouped0", align_bytes=64))
+        nc.vector.tensor_copy(picked_scales[1][:], scales[:].indirect(entries(offs_sb, HALF, HALF)))
+        quantised.append(quantise_weights(1))
+        coords = [product(i, *quantised[i]) for i in range(2)]
 
-        end_a = keep.tile([P, CHUNKS, 2], F32, name="end_a")
+        end_a = keep.tile([P, CHUNKS, 2], F32, name="end_a", tag="grouped1", align_bytes=64)
         nc.scalar.copy(out=end_a[:], in_=ends[0][:, :, 0:2])
         small = {}
-        for name in ("sg", "e", "he"):
+        for name in ("sg", "e", "he", "s2", "es2", "es4"):
             small[name] = keep.tile([P, CHUNKS], F32, name=name)
         nc.vector.tensor_tensor(small["sg"][:], ends[1][:, :, 1], end_a[:, :, 1], ALU.add)
         nc.vector.scalar_tensor_tensor(small["e"][:], ends[1][:, :, 0], -12.0, end_a[:, :, 0], ALU.mult, ALU.mult)
         nc.vector.scalar_tensor_tensor(small["he"][:], ends[1][:, :, 0], -6.0, end_a[:, :, 0], ALU.mult, ALU.mult)
+        nc.vector.tensor_tensor(small["s2"][:], small["sg"][:], small["sg"][:], ALU.mult)
+        nc.vector.tensor_tensor(small["es2"][:], small["e"][:], small["s2"][:], ALU.mult)
+        nc.vector.tensor_tensor(small["es4"][:], small["es2"][:], small["s2"][:], ALU.mult)
 
-        diffs, rsqs, hs = [], [], []
-        for c in range(CHUNKS):
-            first = keep.tile([P, 2, CHUNK], F32, name=f"first{c}", align_bytes=64)
-            diff = keep.tile([P, 2, CHUNK], F32, name=f"diff{c}", align_bytes=64)
+        firsts = [[keep.tile([P, HALF], F32, name=f"first{i}{h}", align_bytes=64) for h in range(2)] for i in range(2)]
+        diffs = [[keep.tile([P, CHUNK], F32, name=f"diff{i}{c}", align_bytes=64) for c in range(CHUNKS)] for i in range(2)]
+
+        def gather_first(i, h):
+            nc.vector.tensor_copy(firsts[i][h][:], coords[i][:].indirect(entries(ia_sb, h * HALF, HALF)))
+
+        def gather_diff(i, c):
+            h, at = divmod(c * CHUNK, HALF)
+            nc.vector.tensor_tensor(
+                diffs[i][c][:], coords[i][:].indirect(entries(ib_sb, c * CHUNK, CHUNK)), firsts[i][h][:, at : at + CHUNK], ALU.subtract
+            )
+
+        def chain(c):
+            squares = [keep.tile([P, CHUNK], F32, name=f"squares{c}{i}", align_bytes=64) for i in range(2)]
             for i in range(2):
-                nc.vector.tensor_copy(first[:, i, :], coords[i][:].indirect(entries(ia_sb, c * CHUNK, CHUNK)))
-            for i in range(2):
-                nc.vector.tensor_tensor(
-                    diff[:, i, :], coords[i][:].indirect(entries(ib_sb, c * CHUNK, CHUNK)), first[:, i, :], ALU.subtract
-                )
-            squares = keep.tile([P, 2, CHUNK], F32, name=f"squares{c}", align_bytes=64)
-            for i in range(2):
-                nc.scalar.activation(squares[:, i, :], diff[:, i, :], ACT.Square)
+                nc.scalar.activation(squares[i][:], diffs[i][c][:], ACT.Square)
             rsq = psum.tile([P, M], F32, name=f"rsq{c}", tag=f"r{c}")
-            terms = (soft[:], squares[:, 0, :], squares[:, 1, :])
+            terms = (soft[:], squares[0][:], squares[1][:])
             for j, term in enumerate(terms):
                 nc.tensor.matmul(rsq[:], term, ident[:], start=(j == 0), stop=(j == len(terms) - 1), is_transpose=True)
             r2 = keep.tile([P, M], F32, name=f"r2_{c}", align_bytes=64)
-            r4 = keep.tile([P, M], F32, name=f"r4_{c}", align_bytes=64)
+            u1 = keep.tile([P, M], F32, name=f"u1_{c}", align_bytes=64)
             u2 = keep.tile([P, M], F32, name=f"u2_{c}", align_bytes=64)
-            h4 = keep.tile([P, M], F32, name=f"h4_{c}", align_bytes=64)
+            u4 = keep.tile([P, M], F32, name=f"u4_{c}", align_bytes=64)
             nc.scalar.activation(r2[:], rsq[:], ACT.Square)
-            nc.scalar.activation(r4[:], r2[:], ACT.Abs_reciprocal_sqrt)
-            nc.scalar.activation(u2[:], r4[:], ACT.Square, scale=small["sg"][:, c : c + 1])
-            nc.scalar.activation(h4[:], u2[:], ACT.Square, scale=small["sg"][:, c : c + 1])
-            diffs.append(diff)
-            rsqs.append(rsq)
-            hs.append(h4)
+            nc.scalar.activation(u1[:], r2[:], ACT.Abs_reciprocal_sqrt)
+            nc.scalar.activation(u2[:], u1[:], ACT.Square, scale=small["sg"][:, c : c + 1])
+            nc.scalar.activation(u4[:], u2[:], ACT.Square, scale=small["sg"][:, c : c + 1])
+            return u1, u2, u4
 
-        for c in range(CHUNKS):
-            q = keep.tile([P, M], F32, name=f"q{c}", align_bytes=64)
+        def finish(c, u1, u2, u4):
+            u3 = keep.tile([P, M], F32, name=f"u3_{c}", align_bytes=64)
             factor = keep.tile([P, M], F32, name=f"factor{c}", align_bytes=64)
-            nc.vector.scalar_tensor_tensor(q[:], rsqs[c][:], small["e"][:, c : c + 1], hs[c][:], ALU.mult, ALU.mult)
-            nc.vector.scalar_tensor_tensor(factor[:], q[:], small["he"][:, c : c + 1], hs[c][:], ALU.subtract, ALU.mult)
+            nc.vector.scalar_tensor_tensor(u3[:], u2[:], small["es4"][:, c : c + 1], u1[:], ALU.mult, ALU.mult)
+            nc.vector.scalar_tensor_tensor(factor[:], u3[:], small["he"][:, c : c + 1], u4[:], ALU.subtract, ALU.mult)
             back = psum.tile([P, CHUNK], F32, name=f"back{c}", tag=f"m{c}")
             nc.tensor.transpose(back[:], factor[:], ident[:])
             force = keep.tile([P, CHUNK], F32, name=f"force{c}", align_bytes=64)
-            nc.vector.tensor_tensor(force[:], back[:], diffs[c][:, 0, :], ALU.mult)
+            nc.vector.tensor_tensor(force[:], back[:], diffs[0][c][:], ALU.mult)
             nc.sync.dma_start(out=out[:, c * CHUNK : (c + 1) * CHUNK], in_=force[:])
+
+        gather_first(0, 0)
+        gather_first(0, 1)
+        powers = []
+        for h in range(2):
+            gather_first(1, h)
+            for c in (2 * h, 2 * h + 1):
+                gather_diff(0, c)
+                gather_diff(1, c)
+                powers.append(chain(c))
+        for c in range(CHUNKS):
+            finish(c, *powers[c])

from contextlib import ExitStack

import concourse.mybir as mybir
from concourse.masks import make_identity

F32 = mybir.dt.float32
BF16 = mybir.dt.bfloat16
I32 = mybir.dt.int32
U32 = mybir.dt.uint32
U16 = mybir.dt.uint16
U8 = mybir.dt.uint8
FP8X4 = mybir.dt.float8_e4m3fn_x4
ALU = mybir.AluOpType
ACT = mybir.ActivationFunctionType

K, T, S, M, U = 512, 2048, 512, 128, 512
P = 128
PACK = 4
LANES = 16
HALF = S // 2
CHUNK = 128
CHUNKS = U // CHUNK
SOFTENING = 0.8
FLOPS = 2 * 2 * K * M * S


def entries(offsets, first, count):
    return offsets[:, first // LANES : (first + count) // LANES]


def tile_picked_yljmix_force_p_kernel(
    tc, x_words, x_scales, w1, w2, eps, sig, offs, ia, ib, out
):
    nc = tc.nc
    with ExitStack() as ctx:
        keep = ctx.enter_context(tc.tile_pool(name="keep", bufs=1))
        psum = ctx.enter_context(tc.psum_pool(name="psum", bufs=1))

        offs_sb = keep.tile([P, S // LANES], U16, name="offs_sb")
        ia_sb = keep.tile([P, U // LANES], U16, name="ia_sb")
        ib_sb = keep.tile([P, U // LANES], U16, name="ib_sb")
        words = keep.tile([P, T], U32, name="words", align_bytes=64)
        scales = keep.tile([P, T], U8, name="scales", align_bytes=64)
        params = keep.tile([P, S], F32, name="params", align_bytes=64)
        w_raw = [keep.tile([P, PACK, M], F32, name=f"w_raw{i}", align_bytes=64) for i in range(2)]

        nc.gpsimd.memset(params[:], 0.0)
        nc.vector.memset(scales[:].bitcast(I32), 0)
        nc.sync.dma_start(offs_sb[:], offs)
        nc.sync.dma_start(ia_sb[:], ia)
        nc.sync.dma_start(ib_sb[:], ib)
        nc.sync.dma_start(out=params[0:1, :], in_=eps[0:1, :])
        nc.sync.dma_start(out=params[1:2, :], in_=sig[0:1, :])
        nc.sync.dma_start(
            out=words[:].bitcast(I32), in_=x_words[0].rearrange("p n t -> p (n t)").bitcast(I32)
        )
        for q in range(4):
            nc.sync.dma_start(
                out=scales[32 * q : 32 * q + 4, :].bitcast(I32),
                in_=x_scales[0, 4 * q : 4 * q + 4, :].bitcast(I32),
            )
        for w, raw in zip((w1, w2), w_raw):
            nc.sync.dma_start(out=raw[:], in_=w.rearrange("(p j) n -> p j n", j=PACK))

        ident = keep.tile([P, P], F32, name="ident", align_bytes=64)
        ones = keep.tile([P, P], F32, name="ones", align_bytes=64)
        nc.vector.memset(ones[:], 1.0)
        make_identity(nc, ident[:])
        soft = keep.tile([P, P], F32, name="soft", align_bytes=64)
        nc.vector.tensor_scalar(soft[:], ones[:], SOFTENING, None, ALU.mult)
        warm = keep.tile([P, 1], F32, name="warm")
        nc.scalar.activation(warm[:], ones[:, 0:1], ACT.Abs_reciprocal_sqrt)


        def look_up_params(name, lst, tag):
            got = keep.tile([P, U], F32, name=f"params_{name}", align_bytes=64)
            for h in range(2):
                nc.vector.tensor_copy(got[:, h * HALF : (h + 1) * HALF], params[:].indirect(entries(lst, h * HALF, HALF)))
            turned = psum.tile([P, CHUNKS, P], F32, name=f"turned_{name}", tag=tag)
            for c in range(CHUNKS):
                nc.tensor.transpose(turned[:, c, :], got[:, c * CHUNK : (c + 1) * CHUNK], ident[:])
            return turned

        def quantise_weights(i):
            grouped = keep.tile([P, M, PACK], BF16, name=f"grouped{i}", tag=f"grouped{i}", align_bytes=64)
            nc.scalar.copy(out=grouped[:], in_=w_raw[i][:].rearrange("p j n -> p n j"))
            w_codes = keep.tile([P, M], U32, name=f"w_codes{i}", align_bytes=64)
            w_scales = keep.tile([P, M], U8, name=f"w_scales{i}", align_bytes=64)
            nc.vector.quantize_mx(
                out=w_codes[:].bitcast(FP8X4), scales=w_scales[:], in_=grouped[:].rearrange("p n j -> p (n j)")
            )
            return w_codes, w_scales

        def product(i, w_codes, w_scales):
            coord = keep.tile([P, S], F32, name=f"coord{i}", align_bytes=64)
            for h in range(2):
                cols = slice(h * HALF, (h + 1) * HALF)
                acc = psum.tile([P, HALF], F32, name=f"acc{i}{h}", tag=f"m{2 * i + h}")
                nc.tensor.matmul_mx(
                    out=acc[:],
                    lhsT=w_codes[:].bitcast(FP8X4),
                    lhsT_scale=w_scales[:],
                    rhs=picked_words[h][:].bitcast(FP8X4),
                    rhs_scale=picked_scales[h][:],
                    start=True,
                    stop=True,
                )
                nc.scalar.copy(out=coord[:, cols], in_=acc[:])
            return coord

        ends = [look_up_params("a", ia_sb, "r2"), look_up_params("b", ib_sb, "r3")]
        picked_words = [keep.tile([P, HALF], U32, name=f"picked_words{h}", align_bytes=64) for h in range(2)]
        picked_scales = [keep.tile([P, HALF], U8, name="picked_scales0", align_bytes=64)]
        nc.vector.tensor_copy(picked_words[0][:], words[:].indirect(entries(offs_sb, 0, HALF)))
        nc.vector.tensor_copy(picked_scales[0][:], scales[:].indirect(entries(offs_sb, 0, HALF)))
        nc.vector.tensor_copy(picked_words[1][:], words[:].indirect(entries(offs_sb, HALF, HALF)))
        quantised = [quantise_weights(0)]
        picked_scales.append(keep.tile([P, HALF], U8, name="picked_scales1", tag="grouped0", align_bytes=64))
        nc.vector.tensor_copy(picked_scales[1][:], scales[:].indirect(entries(offs_sb, HALF, HALF)))
        quantised.append(quantise_weights(1))
        coords = [product(i, *quantised[i]) for i in range(2)]

        end_a = keep.tile([P, CHUNKS, 2], F32, name="end_a", tag="grouped1", align_bytes=64)
        nc.scalar.copy(out=end_a[:], in_=ends[0][:, :, 0:2])
        small = {}
        for name in ("sg", "e", "he", "s2", "es2", "es4"):
            small[name] = keep.tile([P, CHUNKS], F32, name=name)
        nc.vector.tensor_tensor(small["sg"][:], ends[1][:, :, 1], end_a[:, :, 1], ALU.add)
        nc.vector.scalar_tensor_tensor(small["e"][:], ends[1][:, :, 0], -12.0, end_a[:, :, 0], ALU.mult, ALU.mult)
        nc.vector.scalar_tensor_tensor(small["he"][:], ends[1][:, :, 0], -6.0, end_a[:, :, 0], ALU.mult, ALU.mult)
        nc.vector.tensor_tensor(small["s2"][:], small["sg"][:], small["sg"][:], ALU.mult)
        nc.vector.tensor_tensor(small["es2"][:], small["e"][:], small["s2"][:], ALU.mult)
        nc.vector.tensor_tensor(small["es4"][:], small["es2"][:], small["s2"][:], ALU.mult)

        firsts = [[keep.tile([P, HALF], F32, name=f"first{i}{h}", align_bytes=64) for h in range(2)] for i in range(2)]
        diffs = [[keep.tile([P, CHUNK], F32, name=f"diff{i}{c}", align_bytes=64) for c in range(CHUNKS)] for i in range(2)]

        def gather_first(i, h):
            nc.vector.tensor_copy(firsts[i][h][:], coords[i][:].indirect(entries(ia_sb, h * HALF, HALF)))

        def gather_diff(i, c):
            h, at = divmod(c * CHUNK, HALF)
            nc.vector.tensor_tensor(
                diffs[i][c][:], coords[i][:].indirect(entries(ib_sb, c * CHUNK, CHUNK)), firsts[i][h][:, at : at + CHUNK], ALU.subtract
            )

        def chain(c):
            squares = [keep.tile([P, CHUNK], F32, name=f"squares{c}{i}", align_bytes=64) for i in range(2)]
            for i in range(2):
                nc.scalar.activation(squares[i][:], diffs[i][c][:], ACT.Square)
            rsq = psum.tile([P, M], F32, name=f"rsq{c}", tag=f"r{c}")
            terms = (soft[:], squares[0][:], squares[1][:])
            for j, term in enumerate(terms):
                nc.tensor.matmul(rsq[:], term, ident[:], start=(j == 0), stop=(j == len(terms) - 1), is_transpose=True)
            r2 = keep.tile([P, M], F32, name=f"r2_{c}", align_bytes=64)
            u1 = keep.tile([P, M], F32, name=f"u1_{c}", align_bytes=64)
            u2 = keep.tile([P, M], F32, name=f"u2_{c}", align_bytes=64)
            u4 = keep.tile([P, M], F32, name=f"u4_{c}", align_bytes=64)
            nc.scalar.activation(r2[:], rsq[:], ACT.Square)
            nc.scalar.activation(u1[:], r2[:], ACT.Abs_reciprocal_sqrt)
            nc.scalar.activation(u2[:], u1[:], ACT.Square, scale=small["sg"][:, c : c + 1])
            nc.scalar.activation(u4[:], u2[:], ACT.Square, scale=small["sg"][:, c : c + 1])
            return u1, u2, u4

        def finish(c, u1, u2, u4):
            u3 = keep.tile([P, M], F32, name=f"u3_{c}", align_bytes=64)
            factor = keep.tile([P, M], F32, name=f"factor{c}", align_bytes=64)
            nc.vector.scalar_tensor_tensor(u3[:], u2[:], small["es4"][:, c : c + 1], u1[:], ALU.mult, ALU.mult)
            nc.vector.scalar_tensor_tensor(factor[:], u3[:], small["he"][:, c : c + 1], u4[:], ALU.subtract, ALU.mult)
            back = psum.tile([P, CHUNK], F32, name=f"back{c}", tag=f"m{c}")
            nc.tensor.transpose(back[:], factor[:], ident[:])
            force = keep.tile([P, CHUNK], F32, name=f"force{c}", align_bytes=64)
            nc.vector.tensor_tensor(force[:], back[:], diffs[0][c][:], ALU.mult)
            nc.sync.dma_start(out=out[:, c * CHUNK : (c + 1) * CHUNK], in_=force[:])

        gather_first(0, 0)
        gather_first(0, 1)
        powers = []
        for h in range(2):
            gather_first(1, h)
            for c in (2 * h, 2 * h + 1):
                gather_diff(0, c)
                gather_diff(1, c)
                powers.append(chain(c))
        for c in range(CHUNKS):
            finish(c, *powers[c])
